import numpy as np
import ml_dtypes

BF16 = ml_dtypes.bfloat16


def bf(x):
    return np.asarray(x, np.float32).astype(BF16)


def f32(x):
    return np.asarray(x, np.float32)


def f64(x):
    return np.asarray(x).astype(np.float64)


def striped(idx):
    return np.tile(idx.reshape(-1, 16).T, (8, 1))


S, K, M, N, D, V = 1024, 128, 128, 192, 8, 24


def setup_inputs():
    return {"table": bf(np.random.standard_normal((K, S))), "w": bf(np.random.standard_normal((K, M)) / np.sqrt(K)), "b": f32(0.5 * np.random.standard_normal((M, 1))), "offs": striped(np.random.permutation(np.tile(np.arange(S), 2))[:N])}


def reference(table, w, b, offs):
    idx = offs[:16].T.reshape(-1)
    x = f64(table)[:, idx]
    y = f64(w).T @ x
    z = np.tanh(y + f64(b))
    return z.reshape(M, V, D).max(axis=2)

@@ -1,0 +1,43 @@
+import concourse.mybir as mybir
+
+BF16, F32, U16 = mybir.dt.bfloat16, mybir.dt.float32, mybir.dt.uint16
+
+K = 128
+S = 1024
+M = 128
+N = 192
+D = 8
+V = N // D
+
+FLOPS = 2 * K * M * N
+
+
+def tile_gather_matmul_kernel(tc, table, w, b, offs, out):
+    nc = tc.nc
+    with (
+        tc.tile_pool(name="held", bufs=1) as held,
+        tc.psum_pool(name="psum", bufs=1) as psum,
+    ):
+        offsets = held.tile([128, N // 16], U16, name="offsets")
+        nc.sync.dma_start(offsets[:], offs)
+        window = held.tile([K, S], BF16, name="window")
+        nc.sync.dma_start(window[:], table)
+        weights = held.tile([K, M], BF16, name="weights")
+        nc.scalar.dma_start(weights[:], w)
+        bias = held.tile([M, 1], F32, name="bias")
+        nc.scalar.dma_start(bias[:], b)
+
+        product = psum.tile([M, N], F32, name="product")
+        nc.tensor.matmul(product[:], weights[:], window[:].indirect(offsets[:]), start=True, stop=True)
+
+        squashed = held.tile([M, N], F32, name="squashed")
+        nc.scalar.activation(squashed[:], product[:], mybir.ActivationFunctionType.Tanh, bias=bias[:])
+
+        pooled = held.tile([M, V], F32, name="pooled")
+        nc.vector.tensor_reduce(
+            pooled[:],
+            squashed[:].rearrange("m (v t) -> m v t", t=D),
+            mybir.AxisListType.X,
+            mybir.AluOpType.max,
+        )
+        nc.sync.dma_start(out, pooled[:])

@@ -27,6 +27,10 @@ def tile_gather_matmul_kernel(tc, table, w, b, offs, out):
         bias = held.tile([M, 1], F32, name="bias")
         nc.scalar.dma_start(bias[:], b)
 
+        scratch = held.tile([M, 1], F32, name="scratch")
+        nc.vector.memset(scratch[:], 0.0)
+        nc.scalar.activation(scratch[:], scratch[:], mybir.ActivationFunctionType.Tanh)
+
         product = psum.tile([M, N], F32, name="product")
         nc.tensor.matmul(product[:], weights[:], window[:].indirect(offsets[:]), start=True, stop=True)
 

@@ -34,14 +34,14 @@ def tile_gather_matmul_kernel(tc, table, w, b, offs, out):
         product = psum.tile([M, N], F32, name="product")
         nc.tensor.matmul(product[:], weights[:], window[:].indirect(offsets[:]), start=True, stop=True)
 
-        squashed = held.tile([M, N], F32, name="squashed")
-        nc.scalar.activation(squashed[:], product[:], mybir.ActivationFunctionType.Tanh, bias=bias[:])
-
-        pooled = held.tile([M, V], F32, name="pooled")
+        largest = held.tile([M, V], F32, name="largest")
         nc.vector.tensor_reduce(
-            pooled[:],
-            squashed[:].rearrange("m (v t) -> m v t", t=D),
+            largest[:],
+            product[:].rearrange("m (v t) -> m v t", t=D),
             mybir.AxisListType.X,
             mybir.AluOpType.max,
         )
+
+        pooled = held.tile([M, V], F32, name="pooled")
+        nc.scalar.activation(pooled[:], largest[:], mybir.ActivationFunctionType.Tanh, bias=bias[:])
         nc.sync.dma_start(out, pooled[:])

@@ -20,12 +20,12 @@ def tile_gather_matmul_kernel(tc, table, w, b, offs, out):
     ):
         offsets = held.tile([128, N // 16], U16, name="offsets")
         nc.sync.dma_start(offsets[:], offs)
-        window = held.tile([K, S], BF16, name="window")
-        nc.sync.dma_start(window[:], table)
         weights = held.tile([K, M], BF16, name="weights")
         nc.scalar.dma_start(weights[:], w)
+        window = held.tile([K, S], BF16, name="window")
+        nc.sync.dma_start(window[:], table)
         bias = held.tile([M, 1], F32, name="bias")
-        nc.scalar.dma_start(bias[:], b)
+        nc.sync.dma_start(bias[:], b)
 
         scratch = held.tile([M, 1], F32, name="scratch")
         nc.vector.memset(scratch[:], 0.0)

@@ -20,10 +20,10 @@ def tile_gather_matmul_kernel(tc, table, w, b, offs, out):
     ):
         offsets = held.tile([128, N // 16], U16, name="offsets")
         nc.sync.dma_start(offsets[:], offs)
-        weights = held.tile([K, M], BF16, name="weights")
-        nc.scalar.dma_start(weights[:], w)
         window = held.tile([K, S], BF16, name="window")
-        nc.sync.dma_start(window[:], table)
+        nc.scalar.dma_start(window[:], table)
+        weights = held.tile([K, M], BF16, name="weights")
+        nc.sync.dma_start(weights[:], w)
         bias = held.tile([M, 1], F32, name="bias")
         nc.sync.dma_start(bias[:], b)
 

@@ -8,6 +8,7 @@ M = 128
 N = 192
 D = 8
 V = N // D
+PIECES = (128, 64)
 
 FLOPS = 2 * K * M * N
 
@@ -16,7 +17,7 @@ def tile_gather_matmul_kernel(tc, table, w, b, offs, out):
     nc = tc.nc
     with (
         tc.tile_pool(name="held", bufs=1) as held,
-        tc.psum_pool(name="psum", bufs=1) as psum,
+        tc.psum_pool(name="psum", bufs=len(PIECES)) as psum,
     ):
         offsets = held.tile([128, N // 16], U16, name="offsets")
         nc.sync.dma_start(offsets[:], offs)
@@ -31,16 +32,24 @@ def tile_gather_matmul_kernel(tc, table, w, b, offs, out):
         nc.vector.memset(scratch[:], 0.0)
         nc.scalar.activation(scratch[:], scratch[:], mybir.ActivationFunctionType.Tanh)
 
-        product = psum.tile([M, N], F32, name="product")
-        nc.tensor.matmul(product[:], weights[:], window[:].indirect(offsets[:]), start=True, stop=True)
-
         largest = held.tile([M, V], F32, name="largest")
-        nc.vector.tensor_reduce(
-            largest[:],
-            product[:].rearrange("m (v t) -> m v t", t=D),
-            mybir.AxisListType.X,
-            mybir.AluOpType.max,
-        )
+        first = 0
+        for entries in PIECES:
+            product = psum.tile([M, entries], F32, name="product")
+            nc.tensor.matmul(
+                product[:],
+                weights[:],
+                window[:].indirect(offsets[:, first // 16 : (first + entries) // 16]),
+                start=True,
+                stop=True,
+            )
+            nc.vector.tensor_reduce(
+                largest[:, first // D : (first + entries) // D],
+                product[:].rearrange("m (v t) -> m v t", t=D),
+                mybir.AxisListType.X,
+                mybir.AluOpType.max,
+            )
+            first += entries
 
         pooled = held.tile([M, V], F32, name="pooled")
         nc.scalar.activation(pooled[:], largest[:], mybir.ActivationFunctionType.Tanh, bias=bias[:])

@@ -8,6 +8,7 @@ M = 128
 N = 192
 D = 8
 V = N // D
+HALF = M // 2
 PIECES = (128, 64)
 
 FLOPS = 2 * K * M * N
@@ -26,7 +27,8 @@ def tile_gather_matmul_kernel(tc, table, w, b, offs, out):
         weights = held.tile([K, M], BF16, name="weights")
         nc.sync.dma_start(weights[:], w)
         bias = held.tile([M, 1], F32, name="bias")
-        nc.sync.dma_start(bias[:], b)
+        nc.sync.dma_start(bias[0:HALF, :], b[0:HALF, :])
+        nc.scalar.dma_start(bias[HALF:M, :], b[HALF:M, :])
 
         scratch = held.tile([M, 1], F32, name="scratch")
         nc.vector.memset(scratch[:], 0.0)

@@ -20,12 +20,12 @@ def tile_gather_matmul_kernel(tc, table, w, b, offs, out):
         tc.tile_pool(name="held", bufs=1) as held,
         tc.psum_pool(name="psum", bufs=len(PIECES)) as psum,
     ):
+        window = held.tile([K, S], BF16, name="window")
+        nc.sync.dma_start(window[:], table)
         offsets = held.tile([128, N // 16], U16, name="offsets")
         nc.sync.dma_start(offsets[:], offs)
-        window = held.tile([K, S], BF16, name="window")
-        nc.scalar.dma_start(window[:], table)
         weights = held.tile([K, M], BF16, name="weights")
-        nc.sync.dma_start(weights[:], w)
+        nc.scalar.dma_start(weights[:], w)
         bias = held.tile([M, 1], F32, name="bias")
         nc.sync.dma_start(bias[0:HALF, :], b[0:HALF, :])
         nc.scalar.dma_start(bias[HALF:M, :], b[HALF:M, :])

@@ -35,6 +35,7 @@ def tile_gather_matmul_kernel(tc, table, w, b, offs, out):
         nc.scalar.activation(scratch[:], scratch[:], mybir.ActivationFunctionType.Tanh)
 
         largest = held.tile([M, V], F32, name="largest")
+        pooled = held.tile([M, V], F32, name="pooled")
         first = 0
         for entries in PIECES:
             product = psum.tile([M, entries], F32, name="product")
@@ -51,8 +52,12 @@ def tile_gather_matmul_kernel(tc, table, w, b, offs, out):
                 mybir.AxisListType.X,
                 mybir.AluOpType.max,
             )
+            nc.scalar.activation(
+                pooled[:, first // D : (first + entries) // D],
+                largest[:, first // D : (first + entries) // D],
+                mybir.ActivationFunctionType.Tanh,
+                bias=bias[:],
+            )
             first += entries
 
-        pooled = held.tile([M, V], F32, name="pooled")
-        nc.scalar.activation(pooled[:], largest[:], mybir.ActivationFunctionType.Tanh, bias=bias[:])
         nc.sync.dma_start(out, pooled[:])

import concourse.mybir as mybir

BF16, F32, U16 = mybir.dt.bfloat16, mybir.dt.float32, mybir.dt.uint16

K = 128
S = 1024
M = 128
N = 192
D = 8
V = N // D
HALF = M // 2
PIECES = (128, 64)

FLOPS = 2 * K * M * N


def tile_gather_matmul_kernel(tc, table, w, b, offs, out):
    nc = tc.nc
    with (
        tc.tile_pool(name="held", bufs=1) as held,
        tc.psum_pool(name="psum", bufs=len(PIECES)) as psum,
    ):
        window = held.tile([K, S], BF16, name="window")
        nc.sync.dma_start(window[:], table)
        offsets = held.tile([128, N // 16], U16, name="offsets")
        nc.sync.dma_start(offsets[:], offs)
        weights = held.tile([K, M], BF16, name="weights")
        nc.scalar.dma_start(weights[:], w)
        bias = held.tile([M, 1], F32, name="bias")
        nc.sync.dma_start(bias[0:HALF, :], b[0:HALF, :])
        nc.scalar.dma_start(bias[HALF:M, :], b[HALF:M, :])

        scratch = held.tile([M, 1], F32, name="scratch")
        nc.vector.memset(scratch[:], 0.0)
        nc.scalar.activation(scratch[:], scratch[:], mybir.ActivationFunctionType.Tanh)

        largest = held.tile([M, V], F32, name="largest")
        pooled = held.tile([M, V], F32, name="pooled")
        first = 0
        for entries in PIECES:
            product = psum.tile([M, entries], F32, name="product")
            nc.tensor.matmul(
                product[:],
                weights[:],
                window[:].indirect(offsets[:, first // 16 : (first + entries) // 16]),
                start=True,
                stop=True,
            )
            nc.vector.tensor_reduce(
                largest[:, first // D : (first + entries) // D],
                product[:].rearrange("m (v t) -> m v t", t=D),
                mybir.AxisListType.X,
                mybir.AluOpType.max,
            )
            nc.scalar.activation(
                pooled[:, first // D : (first + entries) // D],
                largest[:, first // D : (first + entries) // D],
                mybir.ActivationFunctionType.Tanh,
                bias=bias[:],
            )
            first += entries

        nc.sync.dma_start(out, pooled[:])
